import numpy as np
import ml_dtypes


def mxq(x, axis, fmt="e4m3"):
    dtype, down = {"e4m3": (ml_dtypes.float8_e4m3fn, 7), "e5m2": (ml_dtypes.float8_e5m2, 14)}[fmt]
    v = np.moveaxis(np.asarray(x, np.float32).astype(ml_dtypes.bfloat16).astype(np.float64), axis, -1)
    blocks = v.reshape(v.shape[:-1] + (-1, 32))
    amax = np.abs(blocks).max(-1, keepdims=True)
    byte = np.maximum(np.where(amax > 0, np.frexp(amax)[1] - 1 + 127, 0) - down, 1)
    scale = np.exp2(byte - 127.0)
    codes = (blocks / scale).astype(np.float32).astype(dtype).astype(np.float64)
    return np.moveaxis((codes * scale).reshape(v.shape), -1, axis)


WIDE = False


def mx_kscale(k):
    if not WIDE:
        return np.ones(k)
    levels = np.array([10, -10, 5, -5, 0])
    if k % 512:
        return np.exp2(np.random.permutation(np.resize(levels, k // 32))).repeat(32)
    a = np.empty((k // 512, 16))
    for p in range(k // 512):
        a[p, :8] = np.random.permutation(np.resize(levels, 8))
        for g in range(8):
            far = levels[np.abs(levels - a[p, g]) >= 10]
            a[p, g + 8] = far[np.random.randint(len(far))]
    return np.exp2(a.ravel()).repeat(32)


BF16 = ml_dtypes.bfloat16


def bf(x):
    return np.asarray(x, np.float32).astype(BF16)


def f64(x):
    return np.asarray(x).astype(np.float64)


E2M1 = np.array([0.0, 0.5, 1.0, 1.5, 2.0, 3.0, 4.0, 6.0, -0.0, -0.5, -1.0, -1.5, -2.0, -3.0, -4.0, -6.0])


def pack_weight(w, fmt):
    k, n = w.shape
    w = f64(bf(w)).reshape(k // 32, 32, n)
    amax = np.abs(w).max(1)
    if fmt == "e4m3":
        byte = np.frexp(amax)[1] - 1 + 127 - 7
    else:
        mant, ex = np.frexp(amax / 6.0)
        byte = np.where(mant > 0.5, ex, ex - 1) + 127
    byte = np.clip(np.where(amax > 0, byte, 1), 1, 254)
    scaled = (w * np.exp2(127.0 - byte)[:, None, :]).reshape(k, n).astype(np.float32)
    by_word = np.ascontiguousarray(scaled.reshape(k // 512, 128, 4, n).transpose(0, 1, 3, 2))
    if fmt == "e4m3":
        words = by_word.astype(ml_dtypes.float8_e4m3fn).view(np.uint8)
    else:
        c = by_word.astype(ml_dtypes.float4_e2m1fn).view(np.uint8) & 0xF
        words = c[..., 0::2] | (c[..., 1::2] << 4)
    return np.ascontiguousarray(words), np.ascontiguousarray(byte.astype(np.uint8).reshape(k // 512, 16, n))


def unpack_weight(words, scales, fmt):
    g, p, n, _ = words.shape
    if fmt == "e4m3":
        vals = np.ascontiguousarray(words).view(ml_dtypes.float8_e4m3fn).astype(np.float64)
    else:
        nib = np.empty((g, p, n, 4), np.uint8)
        nib[..., 0::2] = words & 0xF
        nib[..., 1::2] = words >> 4
        vals = E2M1[nib]
    vals = vals * np.repeat(np.exp2(scales.astype(np.float64) - 127.0), 8, axis=1)[..., None]
    return vals.transpose(0, 1, 3, 2).reshape(g * 512, n)
def pack4(w):
    words, scales = pack_weight(w, "e2m1")
    return words.reshape(words.shape[0], 128, -1), scales


def unpack4(words, scales):
    return unpack_weight(words.reshape(words.shape[0], 128, -1, 2), scales, "e2m1")


N, D, H, TWO = 1024, 1024, 1024, 2


def sigmoid(v):
    return 1.0 / (1.0 + np.exp(-v))


def draw0():
    s, t = mx_kscale(D), mx_kscale(H)
    x = bf(np.random.standard_normal((N, D)) * s)
    h = bf(np.random.standard_normal((N, H)))
    wx_words, wx_scales = pack4(np.random.standard_normal((D, H)) / np.sqrt(D) / s[:, None])
    uz_words, uz_scales = pack4(2.0 * np.random.standard_normal((H, H)) / np.sqrt(H) / t[:, None])
    return {
        "x": x,
        "h": h,
        "wx_words": wx_words,
        "wx_scales": wx_scales,
        "uz_words": uz_words,
        "uz_scales": uz_scales,
        "uh": bf(np.random.standard_normal((H, H)) / np.sqrt(H)),
        "bias": bf(np.random.standard_normal((TWO, H)) * 0.4),
        "gain": bf((1.0 + 0.3 * np.random.standard_normal(H)) * t),
    }


def core(x, h, wx_words, wx_scales, uz_words, uz_scales, uh, bias, gain):
    hf = f64(h)
    b = f64(bias)
    z = np.tanh((mxq(f64(x), 1, "e4m3") @ unpack4(wx_words, wx_scales)) + b[0][None, :])
    zg = z * f64(gain)[None, :]
    u = sigmoid(hf @ f64(uh) + (mxq(zg, 1, "e4m3") @ unpack4(uz_words, uz_scales)) + b[1][None, :])
    return u * hf + (1.0 - u) * z


def e4m3fn_bytes(y):
    return np.clip(np.asarray(y, np.float64), -448.0, 448.0).astype(np.float32).astype(ml_dtypes.float8_e4m3fn).view(np.uint8)


def e4m3fn_values(b):
    return np.asarray(b, np.uint8).view(ml_dtypes.float8_e4m3fn).astype(np.float64)


def setup_inputs():
    d = draw0()
    x0 = np.asarray(d['x']).astype(np.float64)
    s = (np.max(np.abs(x0), axis=(0,), keepdims=True) / 448.0).astype(np.float32)
    out = {}
    for k, v in d.items():
        if k == 'x':
            out['x_bytes'] = e4m3fn_bytes(x0 / s.astype(np.float64))
            out['x_scale'] = s
        else:
            out[k] = v
    return out


def reference(x_bytes, x_scale, h, wx_words, wx_scales, uz_words, uz_scales, uh, bias, gain):
    return core(e4m3fn_values(x_bytes) * x_scale.astype(np.float64), h, wx_words, wx_scales, uz_words, uz_scales, uh, bias, gain)

@@ -1,0 +1,366 @@
+from contextlib import ExitStack
+
+import concourse.mybir as mybir
+from concourse.masks import make_identity
+
+N, D, H = 1024, 1024, 1024
+FLOPS = 2 * N * D * H + 2 * 2 * N * H * H
+
+F32 = mybir.dt.float32
+BF16 = mybir.dt.bfloat16
+U8 = mybir.dt.uint8
+U32 = mybir.dt.uint32
+I32 = mybir.dt.int32
+FP8 = mybir.dt.float8_e4m3fn
+FP8X4 = mybir.dt.float8_e4m3fn_x4
+FP4X4 = mybir.dt.float4_e2m1fn_x4
+ALU = mybir.AluOpType
+ACT = mybir.ActivationFunctionType
+
+P = 128
+PACK = 4
+KP = 512
+TOK = 512
+MM_BANKS = 4
+TR_BANKS = 4
+ALL = slice(0, TOK)
+
+
+def tile_minimalrnnlatentblendstep_w4_kernel(
+    tc, x_bytes, x_scale, h, wx_words, wx_scales, uz_words, uz_scales, uh, bias, gain, out
+):
+    nc = tc.nc
+    with ExitStack() as ctx:
+        keep = ctx.enter_context(tc.tile_pool(name="keep", bufs=1))
+        stage = ctx.enter_context(tc.tile_pool(name="stage", bufs=1))
+        psum = ctx.enter_context(tc.psum_pool(name="psum", bufs=1))
+        ctx.enter_context(tc.manual_schedule())
+
+        count = {"mm": 0, "tr": 0}
+
+        def bank(kind):
+            n = count[kind] % (MM_BANKS if kind == "mm" else TR_BANKS)
+            count[kind] = count[kind] + 1
+            return psum.tile([P, 512], F32, name="%s_bank%d" % (kind, n))
+
+        def kept(shape, dtype, name):
+            return keep.tile(shape, dtype, name=name, align_bytes=64)
+
+        ident = kept([P, P], F32, "ident")
+        warm = kept([P, 2], F32, "warm")
+        xs_col = kept([P, 8], F32, "xs_col")
+        xs_all = kept([P, D], F32, "xs_all")
+        bias_sb = kept([P, 4, PACK], BF16, "bias_sb")
+        gain_bf = kept([P, 2, PACK], BF16, "gain_bf")
+        gain_sb = kept([P, 2, PACK], F32, "gain_sb")
+        xb = [kept([P, 4, D], U8, "xbytes%d" % a) for a in range(2)]
+        h_sb = {(a, g): kept([P, 4, KP], BF16, "h%d%d" % (a, g)) for a in range(2) for g in range(2)}
+        hT = {(a, g): kept([P, PACK, TOK], BF16, "hT%d%d" % (a, g)) for a in range(2) for g in range(2)}
+        uh_sb = {(g, j): kept([P, PACK, KP], BF16, "uh%d%d" % (g, j)) for g in range(2) for j in range(2)}
+        raw_words = {w: kept([P, 2, 2 * H], U8, w + "_raw_words") for w in ("wx", "uz")}
+        raw_scales = {w: kept([P, 2, H], U8, w + "_raw_scales") for w in ("wx", "uz")}
+        w_words = {(w, j): kept([P, 2, PACK, 2 * P], U8, "%s_words%d" % (w, j)) for w in ("wx", "uz") for j in range(2)}
+        w_scales = {(w, j): kept([P, 2, PACK, P], U8, "%s_scales%d" % (w, j)) for w in ("wx", "uz") for j in range(2)}
+        codes = {(s, a, g): kept([P, TOK], U32, "%s_codes%d%d" % (s, a, g)) for s in ("x", "zg") for a in range(2) for g in range(2)}
+        scales = {(s, a, g): kept([P, TOK], U8, "%s_mxscales%d%d" % (s, a, g)) for s in ("x", "zg") for a in range(2) for g in range(2)}
+        z = {(a, o): kept([P, TOK], F32, "z%d%d" % (a, o)) for a in range(2) for o in range(8)}
+        s = {(a, o): kept([P, TOK], F32, "s%d%d" % (a, o)) for a in range(2) for o in range(8)}
+        live = {}
+
+        def load_h(a, g):
+            src = h[a * TOK:(a + 1) * TOK, g * KP:(g + 1) * KP].rearrange("(i p) k -> p i k", p=P)
+            nc.sync.dma_start(out=h_sb[a, g][:], in_=src)
+
+        def load_uh(g, j):
+            src = uh[g * KP:(g + 1) * KP, j * KP:(j + 1) * KP].rearrange("(p t) n -> p t n", t=PACK)
+            nc.sync.dma_start(out=uh_sb[g, j][:], in_=src)
+
+        def load_x(a):
+            nc.sync.dma_start(out=xb[a][:], in_=x_bytes[a * TOK:(a + 1) * TOK, :].rearrange("(i p) k -> p i k", p=P))
+
+        def load_weight(w, words, scale_bytes):
+            nc.sync.dma_start(out=raw_words[w][:], in_=words.rearrange("g p n -> p g n"))
+            for q in range(4):
+                src = scale_bytes[:, 4 * q:4 * q + 4, :].rearrange("g r n -> r g n")
+                nc.sync.dma_start(out=raw_scales[w][32 * q:32 * q + 4, :, :].bitcast(I32), in_=src.bitcast(I32))
+
+        def spread_x_scale():
+            for j in range(2):
+                b = bank("tr")
+                for c in range(4):
+                    nc.tensor.transpose(b[:, c * P:(c + 1) * P], xs_col[:, 4 * j + c:4 * j + c + 1].to_broadcast([P, P]), ident[:])
+                nc.scalar.copy(out=xs_all[:].rearrange("q (p c) -> q p c", c=8)[:, :, 4 * j:4 * j + 4],
+                               in_=b[:].rearrange("q (c p) -> q p c", c=4))
+
+        def permute_weight(w, j):
+            nc.vector.tensor_copy(
+                out=w_words[w, j][:].rearrange("p g t (m b) -> p g t m b", b=2),
+                in_=raw_words[w][:, :, j * 2 * KP:(j + 1) * 2 * KP].rearrange("p g (m t b) -> p g t m b", t=PACK, b=2))
+            nc.vector.tensor_copy(
+                out=w_scales[w, j][:],
+                in_=raw_scales[w][:, :, j * KP:(j + 1) * KP].rearrange("p g (m t) -> p g t m", t=PACK))
+
+        def turn_h(a, g, u):
+            b = bank("tr")
+            for i in range(4):
+                nc.tensor.transpose(b[:, i * P:(i + 1) * P], h_sb[a, g][:, i, :].bitcast(F32)[:, u:KP // 2:2], ident[:])
+            nc.scalar.copy(out=hT[a, g][:, 2 * u:2 * u + 2, :], in_=b[:].bitcast(BF16).rearrange("p (r e) -> p e r", e=2))
+
+        def widen_x(a, i):
+            xw = stage.tile([P, D], BF16, name="xw", bufs=4, align_bytes=64)
+            nc.vector.tensor_tensor(out=xw[:], in0=xb[a][:, i, :].bitcast(FP8), in1=xs_all[:], op=ALU.mult)
+            live["xw", i] = xw
+
+        def turn_x(a, g, pair):
+            if pair == 0:
+                live["xg", g] = stage.tile([P, TOK * PACK], BF16, name="xg", bufs=2, align_bytes=64)
+            b = bank("tr")
+            for u in range(2):
+                for ii in range(2):
+                    words = live["xw", 2 * pair + ii][:].bitcast(F32)
+                    nc.tensor.transpose(b[:, (2 * u + ii) * P:(2 * u + ii + 1) * P], words[:, 256 * g + u:256 * (g + 1):2], ident[:])
+            nc.scalar.copy(out=live["xg", g][:, pair * 1024:(pair + 1) * 1024].bitcast(F32).rearrange("p (r u) -> p r u", u=2),
+                           in_=b[:].rearrange("p (u r) -> p r u", u=2))
+
+        def quant_x(a, g):
+            nc.vector.quantize_mx(out=codes["x", a, g][:].bitcast(FP8X4), scales=scales["x", a, g][:], in_=live["xg", g][:])
+
+        def plain(a, o, g, ts=range(PACK), cols=ALL):
+            j, t = divmod(o, PACK)
+            if g == 0 and ts[0] == 0:
+                live["plain", a, o] = bank("mm")
+            for tk in ts:
+                nc.tensor.matmul(out=live["plain", a, o][:, cols], lhsT=uh_sb[g, j][:, tk, t:KP:PACK], rhs=hT[a, g][:, tk, cols],
+                                 start=(g == 0 and tk == 0), stop=(g == 1 and tk == PACK - 1))
+
+        def plain_around(a, o, g, steps):
+            plain(a, o, g, range(0, 2))
+            for step in steps:
+                step[0](*step[1:])
+            plain(a, o, g, range(2, 4))
+
+        def mx(w, act, a, o, kind="mm"):
+            j, t = divmod(o, PACK)
+            b = bank(kind)
+            for g in range(2):
+                nc.tensor.matmul_mx(out=b[:], lhsT=w_words[w, j][:, g, t, :].bitcast(FP4X4), lhsT_scale=w_scales[w, j][:, g, t, :],
+                                    rhs=codes[act, a, g][:].bitcast(FP8X4), rhs_scale=scales[act, a, g][:],
+                                    start=(g == 0), stop=(g == 1))
+            live[w, a, o] = b
+
+        def latent(a, o):
+            j, t = divmod(o, PACK)
+            nc.scalar.activation(out=z[a, o][:], in_=live["wx", a, o][:], func=ACT.Tanh, bias=bias_sb[:, j, t:t + 1])
+
+        def gained(a, o):
+            j, t = divmod(o, PACK)
+            if t == 0:
+                live["zp", j] = stage.tile([P, PACK, TOK], BF16, name="zp", bufs=2, align_bytes=64)
+            nc.scalar.activation(out=live["zp", j][:, t, :], in_=z[a, o][:], func=ACT.Copy, scale=gain_sb[:, j, t:t + 1])
+
+        def gained_v(a, o):
+            j, t = divmod(o, PACK)
+            if t == 0:
+                live["zp", j] = stage.tile([P, PACK, TOK], BF16, name="zp", bufs=2, align_bytes=64)
+            nc.vector.tensor_scalar(out=live["zp", j][:, t, :], in0=z[a, o][:], scalar1=gain_sb[:, j, t:t + 1], scalar2=None, op0=ALU.mult)
+
+        def weave_zg(a, j):
+            zi = stage.tile([P, TOK * PACK], BF16, name="zi", bufs=2, align_bytes=64)
+            nc.vector.tensor_copy(out=zi[:].rearrange("p (c i t) -> p c t i", i=4, t=PACK),
+                                  in_=live["zp", j][:].rearrange("p t (c i) -> p c t i", i=4))
+            live["zi", j] = zi
+
+        def quant_zg(a, j):
+            nc.vector.quantize_mx(out=codes["zg", a, j][:].bitcast(FP8X4), scales=scales["zg", a, j][:], in_=live["zi", j][:])
+
+        def diff(a, o):
+            j, t = divmod(o, PACK)
+            nc.vector.tensor_tensor(out=z[a, o][:], in0=hT[a, j][:, t, :], in1=z[a, o][:], op=ALU.subtract)
+
+        def park(src, a, o):
+            j, t = divmod(o, PACK)
+            nc.scalar.activation(out=s[a, o][:], in_=live[src, a, o][:], func=ACT.Identity, bias=bias_sb[:, 2 + j, t:t + 1])
+
+        def join(src, a, o, cols=ALL):
+            nc.vector.tensor_tensor(out=s[a, o][:, cols], in0=live[src, a, o][:, cols], in1=s[a, o][:, cols], op=ALU.add)
+
+        def gate(a, o, cols=ALL):
+            nc.scalar.activation(out=s[a, o][:, cols], in_=s[a, o][:, cols], func=ACT.Sigmoid, scale=-1.0)
+
+        def weigh(a, o, cols=ALL):
+            nc.vector.tensor_tensor(out=s[a, o][:, cols], in0=s[a, o][:, cols], in1=z[a, o][:, cols], op=ALU.mult)
+
+        def turn_back(a, j, i):
+            b = bank("tr")
+            for t in range(PACK):
+                nc.tensor.transpose(b[:, t * P:(t + 1) * P], s[a, PACK * j + t][:, i * P:(i + 1) * P], ident[:])
+            live["back", a, j, i] = b
+
+        def finish(a, j, i):
+            res = stage.tile([P, KP], F32, name="res", bufs=4)
+            nc.vector.tensor_tensor(out=res[:].rearrange("p (m t) -> p m t", t=PACK),
+                                    in0=h_sb[a, j][:, i, :].rearrange("p (m t) -> p m t", t=PACK),
+                                    in1=live["back", a, j, i][:].rearrange("p (t m) -> p m t", t=PACK), op=ALU.subtract)
+            nc.sync.dma_start(out=out[a * TOK + i * P:a * TOK + (i + 1) * P, j * KP:(j + 1) * KP], in_=res[:])
+
+        nc.scalar.dma_start(out=xs_col[:], in_=x_scale.rearrange("o (p c) -> p (o c)", c=8))
+        make_identity(nc, ident[:])
+        nc.vector.memset(warm[:, 0:1], 0.0)
+        nc.scalar.activation(out=warm[:, 1:2], in_=warm[:, 0:1], func=ACT.Sigmoid)
+        for w in ("wx", "uz"):
+            nc.vector.memset(raw_scales[w][:].rearrange("p g n -> p (g n)").bitcast(I32), 0)
+        load_h(0, 0)
+        load_x(0)
+        load_uh(0, 0)
+        load_h(0, 1)
+        load_weight("wx", wx_words, wx_scales)
+        load_h(1, 0)
+        load_uh(1, 0)
+        nc.sync.dma_start(out=bias_sb[:], in_=bias.rearrange("r (g p t) -> p (r g) t", p=P, t=PACK))
+        nc.sync.dma_start(out=gain_bf[:], in_=gain.rearrange("(g p t) -> p g t", p=P, t=PACK))
+        load_x(1)
+        load_uh(0, 1)
+        load_uh(1, 1)
+        load_weight("uz", uz_words, uz_scales)
+        load_h(1, 1)
+
+        spread_x_scale()
+        for u in range(2):
+            turn_h(0, 0, u)
+        for i in range(4):
+            widen_x(0, i)
+        for tk in range(PACK):
+            for o in range(4):
+                plain(0, o, 0, [tk])
+            if tk == 1:
+                for pair in range(2):
+                    for g in range(2):
+                        turn_x(0, g, pair)
+                for u in range(2):
+                    turn_h(0, 1, u)
+            if tk == 2:
+                for u in range(2):
+                    turn_h(1, 0, u)
+        permute_weight("wx", 0)
+        for g in range(2):
+            quant_x(0, g)
+        nc.vector.tensor_copy(out=gain_sb[:], in_=gain_bf[:])
+        permute_weight("wx", 1)
+        for i in range(4):
+            widen_x(1, i)
+        permute_weight("uz", 0)
+        fill = [(0, 1), (1, 1), (2, 1), (3, 1), (4, 0), (4, 1), (5, 0), (5, 1)]
+        for o in range(8):
+            mx("wx", "x", 0, o, "tr")
+            latent(0, o)
+            if o > 0:
+                gained(0, o - 1)
+            between = {3: [(turn_x, 1, 0, 0), (turn_x, 1, 1, 0)], 4: [(turn_x, 1, 0, 1), (turn_x, 1, 1, 1)]}.get(o, [])
+            if o > 0 and fill[o - 1][1] == 1:
+                park("plain", 0, fill[o - 1][0])
+            plain_around(0, fill[o][0], fill[o][1], between)
+            if o == 4:
+                diff(0, 0)
+                diff(0, 1)
+                weave_zg(0, 0)
+                diff(0, 2)
+                quant_zg(0, 0)
+                for g in range(2):
+                    quant_x(1, g)
+                permute_weight("uz", 1)
+                for oo in range(3, 4):
+                    diff(0, oo)
+        gained(0, 7)
+        diff(0, 4)
+        weave_zg(0, 1)
+        diff(0, 5)
+        quant_zg(0, 1)
+        for oo in range(6, 8):
+            diff(0, oo)
+        for o in range(2):
+            mx("wx", "x", 1, o, "tr")
+            latent(1, o)
+        park("plain", 0, 5)
+        plain_around(0, 6, 0, [(turn_h, 1, 1, 0)])
+        gained(1, 0)
+        fill = [(0, 6, 1), (0, 7, 0), (0, 7, 1), (1, 0, 0), (1, 0, 1), (1, 1, 0), (1, 1, 1), (1, 2, 0)]
+        for o in range(8):
+            mx("uz", "zg", 0, o, "tr")
+            if o < 6:
+                mx("wx", "x", 1, o + 2, "tr")
+            join("uz", 0, o)
+            if o < 6:
+                latent(1, o + 2)
+            if o < 7:
+                gained(1, o + 1)
+            gate(0, o)
+            if o > 0:
+                weigh(0, o - 1)
+            if o in (2, 6):
+                weave_zg(1, o // 4)
+            between = []
+            if o == 0:
+                between = [(turn_h, 1, 1, 1)]
+            if o >= 5:
+                between = [(turn_back, 0, 0, o - 5)]
+            plain_around(fill[o][0], fill[o][1], fill[o][2], between)
+            if fill[o][2] == 1:
+                park("plain", fill[o][0], fill[o][1])
+            if o in (2, 6):
+                diff(1, o // 4)
+                quant_zg(1, o // 4)
+            if o >= 5:
+                finish(0, 0, o - 5)
+            if o in (3, 4):
+                diff(1, o - 1)
+        plain_around(1, 2, 1, [(turn_back, 0, 0, 3)])
+        weigh(0, 7)
+        finish(0, 0, 3)
+        park("plain", 1, 2)
+        for o in range(8):
+            mx("uz", "zg", 1, o, "tr")
+            if o < 3:
+                join("uz", 1, o)
+                gate(1, o)
+            else:
+                park("uz", 1, o)
+            if o in (1, 2, 3):
+                weigh(1, o - 1)
+            if o == 3:
+                plain_around(1, 3, 0, [(turn_back, 0, 1, i) for i in range(2)])
+                for i in range(2):
+                    finish(0, 1, i)
+        plain_around(1, 3, 1, [(turn_back, 0, 1, i) for i in range(2, 4)])
+        finish(0, 1, 2)
+        join("plain", 1, 3)
+        gate(1, 3)
+        finish(0, 1, 3)
+        for half in range(2):
+            cols = slice(256 * half, 256 * half + 256)
+            for o in range(4, 8):
+                plain(1, o, 0, range(4), cols)
+                if half == 0:
+                    diff(1, o)
+                    if o == 4:
+                        weigh(1, 3)
+                    if o > 4:
+                        turn_back(1, 0, o - 5)
+                elif o == 4:
+                    turn_back(1, 0, 3)
+                elif o == 5 or o == 6:
+                    turn_back(1, 1, o - 5)
+                plain(1, o, 1, range(4), cols)
+                if o > 4 or half:
+                    weigh(1, o - 1 if o > 4 else 7, cols if o > 4 else slice(0, 256))
+                join("plain", 1, o, cols)
+                gate(1, o, cols)
+                if half == 0 and o > 4:
+                    finish(1, 0, o - 5)
+                if half and o == 4:
+                    finish(1, 0, 3)
+                if half and o in (5, 6):
+                    finish(1, 1, o - 5)
+        weigh(1, 7, slice(256, 512))
+        for i in range(2, 4):
+            turn_back(1, 1, i)
+            finish(1, 1, i)

@@ -55,7 +55,7 @@ def tile_minimalrnnlatentblendstep_w4_kernel(
         gain_sb = kept([P, 2, PACK], F32, "gain_sb")
         xb = [kept([P, 4, D], U8, "xbytes%d" % a) for a in range(2)]
         h_sb = {(a, g): kept([P, 4, KP], BF16, "h%d%d" % (a, g)) for a in range(2) for g in range(2)}
-        hT = {(a, g): kept([P, PACK, TOK], BF16, "hT%d%d" % (a, g)) for a in range(2) for g in range(2)}
+        hT = {(a, g): kept([P, 2, 2 * TOK], BF16, "hT%d%d" % (a, g)) for a in range(2) for g in range(2)}
         uh_sb = {(g, j): kept([P, PACK, KP], BF16, "uh%d%d" % (g, j)) for g in range(2) for j in range(2)}
         raw_words = {w: kept([P, 2, 2 * H], U8, w + "_raw_words") for w in ("wx", "uz")}
         raw_scales = {w: kept([P, 2, H], U8, w + "_raw_scales") for w in ("wx", "uz")}
@@ -71,9 +71,9 @@ def tile_minimalrnnlatentblendstep_w4_kernel(
             src = h[a * TOK:(a + 1) * TOK, g * KP:(g + 1) * KP].rearrange("(i p) k -> p i k", p=P)
             nc.sync.dma_start(out=h_sb[a, g][:], in_=src)
 
-        def load_uh(g, j):
+        def load_uh(g, j, ts=slice(0, PACK)):
             src = uh[g * KP:(g + 1) * KP, j * KP:(j + 1) * KP].rearrange("(p t) n -> p t n", t=PACK)
-            nc.sync.dma_start(out=uh_sb[g, j][:], in_=src)
+            nc.sync.dma_start(out=uh_sb[g, j][:, ts, :], in_=src[:, ts, :])
 
         def load_x(a):
             nc.sync.dma_start(out=xb[a][:], in_=x_bytes[a * TOK:(a + 1) * TOK, :].rearrange("(i p) k -> p i k", p=P))
@@ -100,16 +100,35 @@ def tile_minimalrnnlatentblendstep_w4_kernel(
                 out=w_scales[w, j][:],
                 in_=raw_scales[w][:, :, j * KP:(j + 1) * KP].rearrange("p g (m t) -> p g t m", t=PACK))
 
+        def sort_h(a, g, copy):
+            hs = stage.tile([P, 4 * KP // 2], F32, name="h_sorted", bufs=2, align_bytes=64)
+            copy(out=hs[:].rearrange("p (i u m) -> p i u m", i=4, u=2),
+                 in_=h_sb[a, g][:].rearrange("p i k -> p (i k)").bitcast(F32).rearrange("p (i m u) -> p i u m", i=4, u=2))
+            live["hs", a, g] = hs
+
         def turn_h(a, g, u):
             b = bank("tr")
             for i in range(4):
-                nc.tensor.transpose(b[:, i * P:(i + 1) * P], h_sb[a, g][:, i, :].bitcast(F32)[:, u:KP // 2:2], ident[:])
-            nc.scalar.copy(out=hT[a, g][:, 2 * u:2 * u + 2, :], in_=b[:].bitcast(BF16).rearrange("p (r e) -> p e r", e=2))
+                if ("hs", a, g) in live:
+                    src = live["hs", a, g][:, (2 * i + u) * P:(2 * i + u + 1) * P]
+                else:
+                    src = h_sb[a, g][:, i, :].bitcast(F32)[:, u:KP // 2:2]
+                nc.tensor.transpose(b[:, i * P:(i + 1) * P], src, ident[:])
+            nc.scalar.copy(out=hT[a, g][:, u, :].bitcast(F32), in_=b[:])
+
+        def h_plane(a, g, t):
+            return hT[a, g][:, t // 2, t % 2:2 * TOK:2]
 
         def widen_x(a, i):
             xw = stage.tile([P, D], BF16, name="xw", bufs=4, align_bytes=64)
             nc.vector.tensor_tensor(out=xw[:], in0=xb[a][:, i, :].bitcast(FP8), in1=xs_all[:], op=ALU.mult)
             live["xw", i] = xw
+
+        def sort_x(a, i, copy):
+            xs = stage.tile([P, D // 2], F32, name="x_sorted", bufs=4, align_bytes=64)
+            copy(out=xs[:].rearrange("p (g u m) -> p g u m", g=2, u=2),
+                 in_=live["xw", i][:].bitcast(F32).rearrange("p (g m u) -> p g u m", g=2, u=2))
+            live["xs", a, i] = xs
 
         def turn_x(a, g, pair):
             if pair == 0:
@@ -117,8 +136,11 @@ def tile_minimalrnnlatentblendstep_w4_kernel(
             b = bank("tr")
             for u in range(2):
                 for ii in range(2):
-                    words = live["xw", 2 * pair + ii][:].bitcast(F32)
-                    nc.tensor.transpose(b[:, (2 * u + ii) * P:(2 * u + ii + 1) * P], words[:, 256 * g + u:256 * (g + 1):2], ident[:])
+                    if ("xs", a, 2 * pair + ii) in live:
+                        src = live["xs", a, 2 * pair + ii][:, (2 * g + u) * P:(2 * g + u + 1) * P]
+                    else:
+                        src = live["xw", 2 * pair + ii][:].bitcast(F32)[:, 256 * g + u:256 * (g + 1):2]
+                    nc.tensor.transpose(b[:, (2 * u + ii) * P:(2 * u + ii + 1) * P], src, ident[:])
             nc.scalar.copy(out=live["xg", g][:, pair * 1024:(pair + 1) * 1024].bitcast(F32).rearrange("p (r u) -> p r u", u=2),
                            in_=b[:].rearrange("p (u r) -> p r u", u=2))
 
@@ -130,7 +152,7 @@ def tile_minimalrnnlatentblendstep_w4_kernel(
             if g == 0 and ts[0] == 0:
                 live["plain", a, o] = bank("mm")
             for tk in ts:
-                nc.tensor.matmul(out=live["plain", a, o][:, cols], lhsT=uh_sb[g, j][:, tk, t:KP:PACK], rhs=hT[a, g][:, tk, cols],
+                nc.tensor.matmul(out=live["plain", a, o][:, cols], lhsT=uh_sb[g, j][:, tk, t:KP:PACK], rhs=h_plane(a, g, tk)[:, cols],
                                  start=(g == 0 and tk == 0), stop=(g == 1 and tk == PACK - 1))
 
         def plain_around(a, o, g, steps):
@@ -175,7 +197,7 @@ def tile_minimalrnnlatentblendstep_w4_kernel(
 
         def diff(a, o):
             j, t = divmod(o, PACK)
-            nc.vector.tensor_tensor(out=z[a, o][:], in0=hT[a, j][:, t, :], in1=z[a, o][:], op=ALU.subtract)
+            nc.vector.tensor_tensor(out=z[a, o][:], in0=h_plane(a, j, t), in1=z[a, o][:], op=ALU.subtract)
 
         def park(src, a, o):
             j, t = divmod(o, PACK)
@@ -187,8 +209,8 @@ def tile_minimalrnnlatentblendstep_w4_kernel(
         def gate(a, o, cols=ALL):
             nc.scalar.activation(out=s[a, o][:, cols], in_=s[a, o][:, cols], func=ACT.Sigmoid, scale=-1.0)
 
-        def weigh(a, o, cols=ALL):
-            nc.vector.tensor_tensor(out=s[a, o][:, cols], in0=s[a, o][:, cols], in1=z[a, o][:, cols], op=ALU.mult)
+        def weigh(a, o, cols=ALL, eng=nc.vector):
+            eng.tensor_tensor(out=s[a, o][:, cols], in0=s[a, o][:, cols], in1=z[a, o][:, cols], op=ALU.mult)
 
         def turn_back(a, j, i):
             b = bank("tr")
@@ -204,86 +226,89 @@ def tile_minimalrnnlatentblendstep_w4_kernel(
             nc.sync.dma_start(out=out[a * TOK + i * P:a * TOK + (i + 1) * P, j * KP:(j + 1) * KP], in_=res[:])
 
         nc.scalar.dma_start(out=xs_col[:], in_=x_scale.rearrange("o (p c) -> p (o c)", c=8))
+        nc.gpsimd.memset(warm[:, 0:1], 0.0)
         make_identity(nc, ident[:])
-        nc.vector.memset(warm[:, 0:1], 0.0)
         nc.scalar.activation(out=warm[:, 1:2], in_=warm[:, 0:1], func=ACT.Sigmoid)
         for w in ("wx", "uz"):
-            nc.vector.memset(raw_scales[w][:].rearrange("p g n -> p (g n)").bitcast(I32), 0)
+            nc.gpsimd.memset(raw_scales[w][:].rearrange("p g n -> p (g n)").bitcast(I32), 0)
         load_h(0, 0)
+        load_uh(0, 0, slice(0, 2))
         load_x(0)
-        load_uh(0, 0)
+        load_uh(0, 0, slice(2, 4))
         load_h(0, 1)
         load_weight("wx", wx_words, wx_scales)
-        load_h(1, 0)
         load_uh(1, 0)
+        load_x(1)
         nc.sync.dma_start(out=bias_sb[:], in_=bias.rearrange("r (g p t) -> p (r g) t", p=P, t=PACK))
         nc.sync.dma_start(out=gain_bf[:], in_=gain.rearrange("(g p t) -> p g t", p=P, t=PACK))
-        load_x(1)
+        load_h(1, 0)
+        load_weight("uz", uz_words, uz_scales)
         load_uh(0, 1)
         load_uh(1, 1)
-        load_weight("uz", uz_words, uz_scales)
         load_h(1, 1)
 
         spread_x_scale()
         for u in range(2):
             turn_h(0, 0, u)
+        sort_h(0, 1, nc.scalar.copy)
         for i in range(4):
             widen_x(0, i)
+            if i > 0:
+                sort_x(0, i - 1, nc.vector.tensor_copy)
+        permute_weight("wx", 0)
         for tk in range(PACK):
             for o in range(4):
                 plain(0, o, 0, [tk])
-            if tk == 1:
-                for pair in range(2):
-                    for g in range(2):
-                        turn_x(0, g, pair)
-                for u in range(2):
-                    turn_h(0, 1, u)
             if tk == 2:
                 for u in range(2):
-                    turn_h(1, 0, u)
-        permute_weight("wx", 0)
+                    turn_h(0, 1, u)
+                sort_x(0, 3, nc.scalar.copy)
+                for g in range(2):
+                    turn_x(0, g, 0)
+        plain_around(0, 0, 1, [(turn_x, 0, 0, 1), (turn_x, 0, 1, 1)])
         for g in range(2):
             quant_x(0, g)
         nc.vector.tensor_copy(out=gain_sb[:], in_=gain_bf[:])
-        permute_weight("wx", 1)
         for i in range(4):
             widen_x(1, i)
+            if i > 0:
+                sort_x(1, i - 1, nc.vector.tensor_copy)
+        permute_weight("wx", 1)
+        sort_x(1, 3, nc.vector.tensor_copy)
         permute_weight("uz", 0)
-        fill = [(0, 1), (1, 1), (2, 1), (3, 1), (4, 0), (4, 1), (5, 0), (5, 1)]
+        plain(0, 1, 1)
+        fill = [(2, 1), (3, 1), (4, 0), (4, 1), (5, 0), (5, 1), (6, 0), (6, 1)]
+        park("plain", 0, 0)
+        park("plain", 0, 1)
         for o in range(8):
-            mx("wx", "x", 0, o, "tr")
-            latent(0, o)
-            if o > 0:
-                gained(0, o - 1)
-            between = {3: [(turn_x, 1, 0, 0), (turn_x, 1, 1, 0)], 4: [(turn_x, 1, 0, 1), (turn_x, 1, 1, 1)]}.get(o, [])
+            for a, oo in {6: [(0, 6), (0, 7)], 7: [(1, 0), (1, 1)]}.get(o, [(0, o)]):
+                mx("wx", "x", a, oo, "tr")
+                latent(a, oo)
+                if (a, oo) != (0, 0):
+                    gained(*((a, oo - 1) if oo else (0, 7)))
+            if o == 7:
+                weave_zg(0, 1)
+            between = {3: [(turn_x, 1, 0, 0), (turn_x, 1, 1, 0)], 4: [(turn_x, 1, 0, 1), (turn_x, 1, 1, 1)], 7: [(turn_h, 1, 0, 0), (turn_h, 1, 0, 1)]}.get(o, [])
             if o > 0 and fill[o - 1][1] == 1:
                 park("plain", 0, fill[o - 1][0])
             plain_around(0, fill[o][0], fill[o][1], between)
             if o == 4:
-                diff(0, 0)
-                diff(0, 1)
                 weave_zg(0, 0)
-                diff(0, 2)
+                diff(0, 0)
                 quant_zg(0, 0)
                 for g in range(2):
                     quant_x(1, g)
-                permute_weight("uz", 1)
-                for oo in range(3, 4):
+                sort_h(1, 0, nc.vector.tensor_copy)
+                sort_h(1, 1, nc.vector.tensor_copy)
+                for oo in range(1, 4):
                     diff(0, oo)
-        gained(0, 7)
         diff(0, 4)
-        weave_zg(0, 1)
-        diff(0, 5)
         quant_zg(0, 1)
-        for oo in range(6, 8):
+        for oo in range(5, 8):
             diff(0, oo)
-        for o in range(2):
-            mx("wx", "x", 1, o, "tr")
-            latent(1, o)
-        park("plain", 0, 5)
-        plain_around(0, 6, 0, [(turn_h, 1, 1, 0)])
-        gained(1, 0)
-        fill = [(0, 6, 1), (0, 7, 0), (0, 7, 1), (1, 0, 0), (1, 0, 1), (1, 1, 0), (1, 1, 1), (1, 2, 0)]
+        park("plain", 0, 6)
+        plain_around(0, 7, 0, [(turn_h, 1, 1, u) for u in range(2)])
+        fill = [(0, 7, 1), (1, 0, 0), (1, 0, 1), (1, 1, 0), (1, 1, 1), (1, 2, 0), (1, 2, 1), (1, 3, 0)]
         for o in range(8):
             mx("uz", "zg", 0, o, "tr")
             if o < 6:
@@ -294,73 +319,52 @@ def tile_minimalrnnlatentblendstep_w4_kernel(
             if o < 7:
                 gained(1, o + 1)
             gate(0, o)
-            if o > 0:
+            if 0 < o <= 6:
                 weigh(0, o - 1)
             if o in (2, 6):
                 weave_zg(1, o // 4)
             between = []
-            if o == 0:
-                between = [(turn_h, 1, 1, 1)]
             if o >= 5:
                 between = [(turn_back, 0, 0, o - 5)]
             plain_around(fill[o][0], fill[o][1], fill[o][2], between)
             if fill[o][2] == 1:
                 park("plain", fill[o][0], fill[o][1])
+            if o == 1:
+                permute_weight("uz", 1)
+            diff(1, o)
             if o in (2, 6):
-                diff(1, o // 4)
                 quant_zg(1, o // 4)
             if o >= 5:
                 finish(0, 0, o - 5)
-            if o in (3, 4):
-                diff(1, o - 1)
-        plain_around(1, 2, 1, [(turn_back, 0, 0, 3)])
-        weigh(0, 7)
+        for o in range(6, 8):
+            weigh(0, o, ALL, nc.gpsimd)
+        plain_around(1, 3, 1, [(turn_back, 0, 0, 3)])
+        park("plain", 1, 3)
         finish(0, 0, 3)
-        park("plain", 1, 2)
-        for o in range(8):
-            mx("uz", "zg", 1, o, "tr")
-            if o < 3:
-                join("uz", 1, o)
-                gate(1, o)
-            else:
-                park("uz", 1, o)
-            if o in (1, 2, 3):
-                weigh(1, o - 1)
-            if o == 3:
-                plain_around(1, 3, 0, [(turn_back, 0, 1, i) for i in range(2)])
-                for i in range(2):
-                    finish(0, 1, i)
-        plain_around(1, 3, 1, [(turn_back, 0, 1, i) for i in range(2, 4)])
-        finish(0, 1, 2)
-        join("plain", 1, 3)
-        gate(1, 3)
-        finish(0, 1, 3)
+        for o in range(4):
+            mx("uz", "zg", 1, o, "tr" if o % 2 else "mm")
+            join("uz", 1, o)
+            gate(1, o)
+            weigh(1, o, ALL, nc.gpsimd)
+        backs = [[(0, 1, 0), (0, 1, 1)], [(0, 1, 2)], [(0, 1, 3)], [(1, 0, 0), (1, 0, 1)], [(1, 0, 2)], [(1, 0, 3)], [(1, 1, 0)], [(1, 1, 1)]]
         for half in range(2):
             cols = slice(256 * half, 256 * half + 256)
             for o in range(4, 8):
-                plain(1, o, 0, range(4), cols)
+                back = backs[4 * half + o - 4]
                 if half == 0:
-                    diff(1, o)
-                    if o == 4:
-                        weigh(1, 3)
-                    if o > 4:
-                        turn_back(1, 0, o - 5)
-                elif o == 4:
-                    turn_back(1, 0, 3)
-                elif o == 5 or o == 6:
-                    turn_back(1, 1, o - 5)
+                    mx("uz", "zg", 1, o, "mm")
+                    park("uz", 1, o)
+                plain(1, o, 0, range(4), cols)
+                for b in back:
+                    turn_back(*b)
                 plain(1, o, 1, range(4), cols)
-                if o > 4 or half:
-                    weigh(1, o - 1 if o > 4 else 7, cols if o > 4 else slice(0, 256))
+                for b in back[1:]:
+                    finish(*b)
                 join("plain", 1, o, cols)
                 gate(1, o, cols)
-                if half == 0 and o > 4:
-                    finish(1, 0, o - 5)
-                if half and o == 4:
-                    finish(1, 0, 3)
-                if half and o in (5, 6):
-                    finish(1, 1, o - 5)
-        weigh(1, 7, slice(256, 512))
+                for b in back[:1]:
+                    finish(*b)
+                weigh(1, o, cols, nc.gpsimd if half == 0 or o < 6 else nc.vector)
         for i in range(2, 4):
             turn_back(1, 1, i)
             finish(1, 1, i)

from contextlib import ExitStack

import concourse.mybir as mybir
from concourse.masks import make_identity

N, D, H = 1024, 1024, 1024
FLOPS = 2 * N * D * H + 2 * 2 * N * H * H

F32 = mybir.dt.float32
BF16 = mybir.dt.bfloat16
U8 = mybir.dt.uint8
U32 = mybir.dt.uint32
I32 = mybir.dt.int32
FP8 = mybir.dt.float8_e4m3fn
FP8X4 = mybir.dt.float8_e4m3fn_x4
FP4X4 = mybir.dt.float4_e2m1fn_x4
ALU = mybir.AluOpType
ACT = mybir.ActivationFunctionType

P = 128
PACK = 4
KP = 512
TOK = 512
MM_BANKS = 4
TR_BANKS = 4
ALL = slice(0, TOK)


def tile_minimalrnnlatentblendstep_w4_kernel(
    tc, x_bytes, x_scale, h, wx_words, wx_scales, uz_words, uz_scales, uh, bias, gain, out
):
    nc = tc.nc
    with ExitStack() as ctx:
        keep = ctx.enter_context(tc.tile_pool(name="keep", bufs=1))
        stage = ctx.enter_context(tc.tile_pool(name="stage", bufs=1))
        psum = ctx.enter_context(tc.psum_pool(name="psum", bufs=1))
        ctx.enter_context(tc.manual_schedule())

        count = {"mm": 0, "tr": 0}

        def bank(kind):
            n = count[kind] % (MM_BANKS if kind == "mm" else TR_BANKS)
            count[kind] = count[kind] + 1
            return psum.tile([P, 512], F32, name="%s_bank%d" % (kind, n))

        def kept(shape, dtype, name):
            return keep.tile(shape, dtype, name=name, align_bytes=64)

        ident = kept([P, P], F32, "ident")
        warm = kept([P, 2], F32, "warm")
        xs_col = kept([P, 8], F32, "xs_col")
        xs_all = kept([P, D], F32, "xs_all")
        bias_sb = kept([P, 4, PACK], BF16, "bias_sb")
        gain_bf = kept([P, 2, PACK], BF16, "gain_bf")
        gain_sb = kept([P, 2, PACK], F32, "gain_sb")
        xb = [kept([P, 4, D], U8, "xbytes%d" % a) for a in range(2)]
        h_sb = {(a, g): kept([P, 4, KP], BF16, "h%d%d" % (a, g)) for a in range(2) for g in range(2)}
        hT = {(a, g): kept([P, 2, 2 * TOK], BF16, "hT%d%d" % (a, g)) for a in range(2) for g in range(2)}
        uh_sb = {(g, j): kept([P, PACK, KP], BF16, "uh%d%d" % (g, j)) for g in range(2) for j in range(2)}
        raw_words = {w: kept([P, 2, 2 * H], U8, w + "_raw_words") for w in ("wx", "uz")}
        raw_scales = {w: kept([P, 2, H], U8, w + "_raw_scales") for w in ("wx", "uz")}
        w_words = {(w, j): kept([P, 2, PACK, 2 * P], U8, "%s_words%d" % (w, j)) for w in ("wx", "uz") for j in range(2)}
        w_scales = {(w, j): kept([P, 2, PACK, P], U8, "%s_scales%d" % (w, j)) for w in ("wx", "uz") for j in range(2)}
        codes = {(s, a, g): kept([P, TOK], U32, "%s_codes%d%d" % (s, a, g)) for s in ("x", "zg") for a in range(2) for g in range(2)}
        scales = {(s, a, g): kept([P, TOK], U8, "%s_mxscales%d%d" % (s, a, g)) for s in ("x", "zg") for a in range(2) for g in range(2)}
        z = {(a, o): kept([P, TOK], F32, "z%d%d" % (a, o)) for a in range(2) for o in range(8)}
        s = {(a, o): kept([P, TOK], F32, "s%d%d" % (a, o)) for a in range(2) for o in range(8)}
        live = {}

        def load_h(a, g):
            src = h[a * TOK:(a + 1) * TOK, g * KP:(g + 1) * KP].rearrange("(i p) k -> p i k", p=P)
            nc.sync.dma_start(out=h_sb[a, g][:], in_=src)

        def load_uh(g, j, ts=slice(0, PACK)):
            src = uh[g * KP:(g + 1) * KP, j * KP:(j + 1) * KP].rearrange("(p t) n -> p t n", t=PACK)
            nc.sync.dma_start(out=uh_sb[g, j][:, ts, :], in_=src[:, ts, :])

        def load_x(a):
            nc.sync.dma_start(out=xb[a][:], in_=x_bytes[a * TOK:(a + 1) * TOK, :].rearrange("(i p) k -> p i k", p=P))

        def load_weight(w, words, scale_bytes):
            nc.sync.dma_start(out=raw_words[w][:], in_=words.rearrange("g p n -> p g n"))
            for q in range(4):
                src = scale_bytes[:, 4 * q:4 * q + 4, :].rearrange("g r n -> r g n")
                nc.sync.dma_start(out=raw_scales[w][32 * q:32 * q + 4, :, :].bitcast(I32), in_=src.bitcast(I32))

        def spread_x_scale():
            for j in range(2):
                b = bank("tr")
                for c in range(4):
                    nc.tensor.transpose(b[:, c * P:(c + 1) * P], xs_col[:, 4 * j + c:4 * j + c + 1].to_broadcast([P, P]), ident[:])
                nc.scalar.copy(out=xs_all[:].rearrange("q (p c) -> q p c", c=8)[:, :, 4 * j:4 * j + 4],
                               in_=b[:].rearrange("q (c p) -> q p c", c=4))

        def permute_weight(w, j):
            nc.vector.tensor_copy(
                out=w_words[w, j][:].rearrange("p g t (m b) -> p g t m b", b=2),
                in_=raw_words[w][:, :, j * 2 * KP:(j + 1) * 2 * KP].rearrange("p g (m t b) -> p g t m b", t=PACK, b=2))
            nc.vector.tensor_copy(
                out=w_scales[w, j][:],
                in_=raw_scales[w][:, :, j * KP:(j + 1) * KP].rearrange("p g (m t) -> p g t m", t=PACK))

        def sort_h(a, g, copy):
            hs = stage.tile([P, 4 * KP // 2], F32, name="h_sorted", bufs=2, align_bytes=64)
            copy(out=hs[:].rearrange("p (i u m) -> p i u m", i=4, u=2),
                 in_=h_sb[a, g][:].rearrange("p i k -> p (i k)").bitcast(F32).rearrange("p (i m u) -> p i u m", i=4, u=2))
            live["hs", a, g] = hs

        def turn_h(a, g, u):
            b = bank("tr")
            for i in range(4):
                if ("hs", a, g) in live:
                    src = live["hs", a, g][:, (2 * i + u) * P:(2 * i + u + 1) * P]
                else:
                    src = h_sb[a, g][:, i, :].bitcast(F32)[:, u:KP // 2:2]
                nc.tensor.transpose(b[:, i * P:(i + 1) * P], src, ident[:])
            nc.scalar.copy(out=hT[a, g][:, u, :].bitcast(F32), in_=b[:])

        def h_plane(a, g, t):
            return hT[a, g][:, t // 2, t % 2:2 * TOK:2]

        def widen_x(a, i):
            xw = stage.tile([P, D], BF16, name="xw", bufs=4, align_bytes=64)
            nc.vector.tensor_tensor(out=xw[:], in0=xb[a][:, i, :].bitcast(FP8), in1=xs_all[:], op=ALU.mult)
            live["xw", i] = xw

        def sort_x(a, i, copy):
            xs = stage.tile([P, D // 2], F32, name="x_sorted", bufs=4, align_bytes=64)
            copy(out=xs[:].rearrange("p (g u m) -> p g u m", g=2, u=2),
                 in_=live["xw", i][:].bitcast(F32).rearrange("p (g m u) -> p g u m", g=2, u=2))
            live["xs", a, i] = xs

        def turn_x(a, g, pair):
            if pair == 0:
                live["xg", g] = stage.tile([P, TOK * PACK], BF16, name="xg", bufs=2, align_bytes=64)
            b = bank("tr")
            for u in range(2):
                for ii in range(2):
                    if ("xs", a, 2 * pair + ii) in live:
                        src = live["xs", a, 2 * pair + ii][:, (2 * g + u) * P:(2 * g + u + 1) * P]
                    else:
                        src = live["xw", 2 * pair + ii][:].bitcast(F32)[:, 256 * g + u:256 * (g + 1):2]
                    nc.tensor.transpose(b[:, (2 * u + ii) * P:(2 * u + ii + 1) * P], src, ident[:])
            nc.scalar.copy(out=live["xg", g][:, pair * 1024:(pair + 1) * 1024].bitcast(F32).rearrange("p (r u) -> p r u", u=2),
                           in_=b[:].rearrange("p (u r) -> p r u", u=2))

        def quant_x(a, g):
            nc.vector.quantize_mx(out=codes["x", a, g][:].bitcast(FP8X4), scales=scales["x", a, g][:], in_=live["xg", g][:])

        def plain(a, o, g, ts=range(PACK), cols=ALL):
            j, t = divmod(o, PACK)
            if g == 0 and ts[0] == 0:
                live["plain", a, o] = bank("mm")
            for tk in ts:
                nc.tensor.matmul(out=live["plain", a, o][:, cols], lhsT=uh_sb[g, j][:, tk, t:KP:PACK], rhs=h_plane(a, g, tk)[:, cols],
                                 start=(g == 0 and tk == 0), stop=(g == 1 and tk == PACK - 1))

        def plain_around(a, o, g, steps):
            plain(a, o, g, range(0, 2))
            for step in steps:
                step[0](*step[1:])
            plain(a, o, g, range(2, 4))

        def mx(w, act, a, o, kind="mm"):
            j, t = divmod(o, PACK)
            b = bank(kind)
            for g in range(2):
                nc.tensor.matmul_mx(out=b[:], lhsT=w_words[w, j][:, g, t, :].bitcast(FP4X4), lhsT_scale=w_scales[w, j][:, g, t, :],
                                    rhs=codes[act, a, g][:].bitcast(FP8X4), rhs_scale=scales[act, a, g][:],
                                    start=(g == 0), stop=(g == 1))
            live[w, a, o] = b

        def latent(a, o):
            j, t = divmod(o, PACK)
            nc.scalar.activation(out=z[a, o][:], in_=live["wx", a, o][:], func=ACT.Tanh, bias=bias_sb[:, j, t:t + 1])

        def gained(a, o):
            j, t = divmod(o, PACK)
            if t == 0:
                live["zp", j] = stage.tile([P, PACK, TOK], BF16, name="zp", bufs=2, align_bytes=64)
            nc.scalar.activation(out=live["zp", j][:, t, :], in_=z[a, o][:], func=ACT.Copy, scale=gain_sb[:, j, t:t + 1])

        def gained_v(a, o):
            j, t = divmod(o, PACK)
            if t == 0:
                live["zp", j] = stage.tile([P, PACK, TOK], BF16, name="zp", bufs=2, align_bytes=64)
            nc.vector.tensor_scalar(out=live["zp", j][:, t, :], in0=z[a, o][:], scalar1=gain_sb[:, j, t:t + 1], scalar2=None, op0=ALU.mult)

        def weave_zg(a, j):
            zi = stage.tile([P, TOK * PACK], BF16, name="zi", bufs=2, align_bytes=64)
            nc.vector.tensor_copy(out=zi[:].rearrange("p (c i t) -> p c t i", i=4, t=PACK),
                                  in_=live["zp", j][:].rearrange("p t (c i) -> p c t i", i=4))
            live["zi", j] = zi

        def quant_zg(a, j):
            nc.vector.quantize_mx(out=codes["zg", a, j][:].bitcast(FP8X4), scales=scales["zg", a, j][:], in_=live["zi", j][:])

        def diff(a, o):
            j, t = divmod(o, PACK)
            nc.vector.tensor_tensor(out=z[a, o][:], in0=h_plane(a, j, t), in1=z[a, o][:], op=ALU.subtract)

        def park(src, a, o):
            j, t = divmod(o, PACK)
            nc.scalar.activation(out=s[a, o][:], in_=live[src, a, o][:], func=ACT.Identity, bias=bias_sb[:, 2 + j, t:t + 1])

        def join(src, a, o, cols=ALL):
            nc.vector.tensor_tensor(out=s[a, o][:, cols], in0=live[src, a, o][:, cols], in1=s[a, o][:, cols], op=ALU.add)

        def gate(a, o, cols=ALL):
            nc.scalar.activation(out=s[a, o][:, cols], in_=s[a, o][:, cols], func=ACT.Sigmoid, scale=-1.0)

        def weigh(a, o, cols=ALL, eng=nc.vector):
            eng.tensor_tensor(out=s[a, o][:, cols], in0=s[a, o][:, cols], in1=z[a, o][:, cols], op=ALU.mult)

        def turn_back(a, j, i):
            b = bank("tr")
            for t in range(PACK):
                nc.tensor.transpose(b[:, t * P:(t + 1) * P], s[a, PACK * j + t][:, i * P:(i + 1) * P], ident[:])
            live["back", a, j, i] = b

        def finish(a, j, i):
            res = stage.tile([P, KP], F32, name="res", bufs=4)
            nc.vector.tensor_tensor(out=res[:].rearrange("p (m t) -> p m t", t=PACK),
                                    in0=h_sb[a, j][:, i, :].rearrange("p (m t) -> p m t", t=PACK),
                                    in1=live["back", a, j, i][:].rearrange("p (t m) -> p m t", t=PACK), op=ALU.subtract)
            nc.sync.dma_start(out=out[a * TOK + i * P:a * TOK + (i + 1) * P, j * KP:(j + 1) * KP], in_=res[:])

        nc.scalar.dma_start(out=xs_col[:], in_=x_scale.rearrange("o (p c) -> p (o c)", c=8))
        nc.gpsimd.memset(warm[:, 0:1], 0.0)
        make_identity(nc, ident[:])
        nc.scalar.activation(out=warm[:, 1:2], in_=warm[:, 0:1], func=ACT.Sigmoid)
        for w in ("wx", "uz"):
            nc.gpsimd.memset(raw_scales[w][:].rearrange("p g n -> p (g n)").bitcast(I32), 0)
        load_h(0, 0)
        load_uh(0, 0, slice(0, 2))
        load_x(0)
        load_uh(0, 0, slice(2, 4))
        load_h(0, 1)
        load_weight("wx", wx_words, wx_scales)
        load_uh(1, 0)
        load_x(1)
        nc.sync.dma_start(out=bias_sb[:], in_=bias.rearrange("r (g p t) -> p (r g) t", p=P, t=PACK))
        nc.sync.dma_start(out=gain_bf[:], in_=gain.rearrange("(g p t) -> p g t", p=P, t=PACK))
        load_h(1, 0)
        load_weight("uz", uz_words, uz_scales)
        load_uh(0, 1)
        load_uh(1, 1)
        load_h(1, 1)

        spread_x_scale()
        for u in range(2):
            turn_h(0, 0, u)
        sort_h(0, 1, nc.scalar.copy)
        for i in range(4):
            widen_x(0, i)
            if i > 0:
                sort_x(0, i - 1, nc.vector.tensor_copy)
        permute_weight("wx", 0)
        for tk in range(PACK):
            for o in range(4):
                plain(0, o, 0, [tk])
            if tk == 2:
                for u in range(2):
                    turn_h(0, 1, u)
                sort_x(0, 3, nc.scalar.copy)
                for g in range(2):
                    turn_x(0, g, 0)
        plain_around(0, 0, 1, [(turn_x, 0, 0, 1), (turn_x, 0, 1, 1)])
        for g in range(2):
            quant_x(0, g)
        nc.vector.tensor_copy(out=gain_sb[:], in_=gain_bf[:])
        for i in range(4):
            widen_x(1, i)
            if i > 0:
                sort_x(1, i - 1, nc.vector.tensor_copy)
        permute_weight("wx", 1)
        sort_x(1, 3, nc.vector.tensor_copy)
        permute_weight("uz", 0)
        plain(0, 1, 1)
        fill = [(2, 1), (3, 1), (4, 0), (4, 1), (5, 0), (5, 1), (6, 0), (6, 1)]
        park("plain", 0, 0)
        park("plain", 0, 1)
        for o in range(8):
            for a, oo in {6: [(0, 6), (0, 7)], 7: [(1, 0), (1, 1)]}.get(o, [(0, o)]):
                mx("wx", "x", a, oo, "tr")
                latent(a, oo)
                if (a, oo) != (0, 0):
                    gained(*((a, oo - 1) if oo else (0, 7)))
            if o == 7:
                weave_zg(0, 1)
            between = {3: [(turn_x, 1, 0, 0), (turn_x, 1, 1, 0)], 4: [(turn_x, 1, 0, 1), (turn_x, 1, 1, 1)], 7: [(turn_h, 1, 0, 0), (turn_h, 1, 0, 1)]}.get(o, [])
            if o > 0 and fill[o - 1][1] == 1:
                park("plain", 0, fill[o - 1][0])
            plain_around(0, fill[o][0], fill[o][1], between)
            if o == 4:
                weave_zg(0, 0)
                diff(0, 0)
                quant_zg(0, 0)
                for g in range(2):
                    quant_x(1, g)
                sort_h(1, 0, nc.vector.tensor_copy)
                sort_h(1, 1, nc.vector.tensor_copy)
                for oo in range(1, 4):
                    diff(0, oo)
        diff(0, 4)
        quant_zg(0, 1)
        for oo in range(5, 8):
            diff(0, oo)
        park("plain", 0, 6)
        plain_around(0, 7, 0, [(turn_h, 1, 1, u) for u in range(2)])
        fill = [(0, 7, 1), (1, 0, 0), (1, 0, 1), (1, 1, 0), (1, 1, 1), (1, 2, 0), (1, 2, 1), (1, 3, 0)]
        for o in range(8):
            mx("uz", "zg", 0, o, "tr")
            if o < 6:
                mx("wx", "x", 1, o + 2, "tr")
            join("uz", 0, o)
            if o < 6:
                latent(1, o + 2)
            if o < 7:
                gained(1, o + 1)
            gate(0, o)
            if 0 < o <= 6:
                weigh(0, o - 1)
            if o in (2, 6):
                weave_zg(1, o // 4)
            between = []
            if o >= 5:
                between = [(turn_back, 0, 0, o - 5)]
            plain_around(fill[o][0], fill[o][1], fill[o][2], between)
            if fill[o][2] == 1:
                park("plain", fill[o][0], fill[o][1])
            if o == 1:
                permute_weight("uz", 1)
            diff(1, o)
            if o in (2, 6):
                quant_zg(1, o // 4)
            if o >= 5:
                finish(0, 0, o - 5)
        for o in range(6, 8):
            weigh(0, o, ALL, nc.gpsimd)
        plain_around(1, 3, 1, [(turn_back, 0, 0, 3)])
        park("plain", 1, 3)
        finish(0, 0, 3)
        for o in range(4):
            mx("uz", "zg", 1, o, "tr" if o % 2 else "mm")
            join("uz", 1, o)
            gate(1, o)
            weigh(1, o, ALL, nc.gpsimd)
        backs = [[(0, 1, 0), (0, 1, 1)], [(0, 1, 2)], [(0, 1, 3)], [(1, 0, 0), (1, 0, 1)], [(1, 0, 2)], [(1, 0, 3)], [(1, 1, 0)], [(1, 1, 1)]]
        for half in range(2):
            cols = slice(256 * half, 256 * half + 256)
            for o in range(4, 8):
                back = backs[4 * half + o - 4]
                if half == 0:
                    mx("uz", "zg", 1, o, "mm")
                    park("uz", 1, o)
                plain(1, o, 0, range(4), cols)
                for b in back:
                    turn_back(*b)
                plain(1, o, 1, range(4), cols)
                for b in back[1:]:
                    finish(*b)
                join("plain", 1, o, cols)
                gate(1, o, cols)
                for b in back[:1]:
                    finish(*b)
                weigh(1, o, cols, nc.gpsimd if half == 0 or o < 6 else nc.vector)
        for i in range(2, 4):
            turn_back(1, 1, i)
            finish(1, 1, i)
